import numpy as np
import ml_dtypes


def mxq(x, axis, fmt="e4m3"):
    dtype, down = {"e4m3": (ml_dtypes.float8_e4m3fn, 7), "e5m2": (ml_dtypes.float8_e5m2, 14)}[fmt]
    v = np.moveaxis(np.asarray(x, np.float32).astype(ml_dtypes.bfloat16).astype(np.float64), axis, -1)
    blocks = v.reshape(v.shape[:-1] + (-1, 32))
    amax = np.abs(blocks).max(-1, keepdims=True)
    byte = np.maximum(np.where(amax > 0, np.frexp(amax)[1] - 1 + 127, 0) - down, 1)
    scale = np.exp2(byte - 127.0)
    codes = (blocks / scale).astype(np.float32).astype(dtype).astype(np.float64)
    return np.moveaxis((codes * scale).reshape(v.shape), -1, axis)


WIDE = False


def mx_kscale(k):
    if not WIDE:
        return np.ones(k)
    levels = np.array([10, -10, 5, -5, 0])
    if k % 512:
        return np.exp2(np.random.permutation(np.resize(levels, k // 32))).repeat(32)
    a = np.empty((k // 512, 16))
    for p in range(k // 512):
        a[p, :8] = np.random.permutation(np.resize(levels, 8))
        for g in range(8):
            far = levels[np.abs(levels - a[p, g]) >= 10]
            a[p, g + 8] = far[np.random.randint(len(far))]
    return np.exp2(a.ravel()).repeat(32)


def f64(x):
    return np.asarray(x).astype(np.float64)


def striped(idx):
    return np.tile(idx.reshape(-1, 16).T, (8, 1)).astype(np.uint16)


def unstriped(offs):
    return offs[:16].T.reshape(-1).astype(np.int64)


def pack_weight(w):
    k, n = w.shape
    w = f64(np.asarray(w, np.float32).astype(ml_dtypes.bfloat16)).reshape(k // 32, 32, n)
    amax = np.abs(w).max(1)
    byte = np.clip(np.where(amax > 0, np.frexp(amax)[1] - 1 + 127 - 7, 1), 1, 254)
    scaled = (w * np.exp2(127.0 - byte)[:, None, :]).reshape(k, n).astype(np.float32)
    words = np.ascontiguousarray(scaled.reshape(k // 512, 128, 4, n).transpose(0, 1, 3, 2)).astype(ml_dtypes.float8_e4m3fn).view(np.uint8)
    return words, np.ascontiguousarray(byte.astype(np.uint8).reshape(k // 512, 16, n))


def unpack_weight(words, scales):
    g, p, n, _ = words.shape
    vals = np.ascontiguousarray(words).view(ml_dtypes.float8_e4m3fn).astype(np.float64) * np.repeat(np.exp2(scales.astype(np.float64) - 127.0), 8, axis=1)[..., None]
    return vals.transpose(0, 1, 3, 2).reshape(g * 512, n)


K, T, S, N, U = 1024, 1024, 512, 128, 512
P = 2 ** 7


def setup_inputs():
    n = np.random.standard_normal
    s = mx_kscale(K)[:, None]
    packed_xT = pack_weight(n((K, T)) * s)
    return {
        "x_words": packed_xT[0],
        "x_scales": packed_xT[1],
        "w1": (n((K, N)) / np.sqrt(K) / s).astype(np.float32),
        "will": (np.tile(np.random.uniform(0.5, 2.0, U), (P, 1))).astype(np.float32),
        "peak": (np.tile(np.random.uniform(0.4, 2.0, U), (P, 1))).astype(np.float32),
        "offs": striped(np.random.permutation(T)[:S]),
        "lnk1": striped(np.random.randint(0, S, U)),
        "lnk2": striped(np.random.randint(0, S, U)),
        "lnk3": striped(np.random.randint(0, S, U)),
    }


def reference(x_words, x_scales, w1, will, peak, offs, lnk1, lnk2, lnk3):
    xq = unpack_weight(x_words, x_scales)[:, unstriped(offs)]
    y = mxq(f64(w1), 0, "e4m3").T @ xq
    price = 0.6 * (np.log(np.exp(y) + 1.0))
    path = price[:, unstriped(lnk1)] + price[:, unstriped(lnk2)] + price[:, unstriped(lnk3)]
    rate = np.minimum(f64(will)[:1] / (path + 0.1), f64(peak)[:1])
    return f64(will)[:1] * np.log(rate) - (rate * path)

@@ -1,0 +1,174 @@
+from contextlib import ExitStack
+
+import concourse.mybir as mybir
+
+F32 = mybir.dt.float32
+BF16 = mybir.dt.bfloat16
+I32 = mybir.dt.int32
+U32 = mybir.dt.uint32
+U16 = mybir.dt.uint16
+U8 = mybir.dt.uint8
+FP8X4 = mybir.dt.float8_e4m3fn_x4
+ALU = mybir.AluOpType
+ACT = mybir.ActivationFunctionType
+
+P = 128
+PACK = 4
+PASSES = 2
+T = 1024
+S = 512
+U = 512
+M = 128
+PER_COL = 16
+FLOPS = 2 * PASSES * P * PACK * M * S
+
+LINK_PIECES = ((0, 256), (256, 384), (384, 512))
+FLOW_PIECES = ((0, 256), (256, 512))
+EXP_CAP = 2.0 ** 60
+TINY = 1e-18
+
+
+def cols(piece):
+    return slice(piece[0], piece[1])
+
+
+def list_cols(piece):
+    return slice(piece[0] // PER_COL, piece[1] // PER_COL)
+
+
+def tile_picked_ynumdl_util_p_kernel(
+    tc, x_words, x_scales, w1, will, peak, offs, lnk1, lnk2, lnk3, out
+):
+    nc = tc.nc
+    with ExitStack() as ctx:
+        keep = ctx.enter_context(tc.tile_pool(name="keep", bufs=1))
+        psum = ctx.enter_context(tc.psum_pool(name="psum", bufs=1))
+
+        offs_t = keep.tile([P, S // PER_COL], U16, name="offs_t")
+        lnk_t = [keep.tile([P, U // PER_COL], U16, name="lnk_t%d" % i) for i in range(3)]
+        w_raw = keep.tile([P, PASSES, PACK, M], F32, name="w_raw")
+        words = [keep.tile([P, T], U32, name="words%d" % g, align_bytes=64) for g in range(PASSES)]
+        scales = keep.tile([P, T], U8, name="scales", align_bytes=64)
+        will_t = keep.tile([P, U], F32, name="will_t")
+        peak_t = keep.tile([P, U], F32, name="peak_t")
+
+        nc.vector.memset(scales[:].bitcast(I32), 0)
+        nc.sync.dma_start(offs_t[:], offs)
+        nc.sync.dma_start(words[0][:].bitcast(I32), x_words[0].rearrange("p n t -> p (n t)").bitcast(I32))
+        for q in range(4):
+            nc.sync.dma_start(
+                scales[32 * q : 32 * q + 8, :].bitcast(I32), x_scales[:, 4 * q : 4 * q + 4, :].bitcast(I32)
+            )
+        nc.sync.dma_start(w_raw[:], w1.rearrange("(g p j) m -> p g j m", g=PASSES, j=PACK))
+        nc.sync.dma_start(words[1][:].bitcast(I32), x_words[1].rearrange("p n t -> p (n t)").bitcast(I32))
+        for tile, lnk in zip(lnk_t, (lnk1, lnk2, lnk3)):
+            nc.sync.dma_start(tile[:], lnk)
+        nc.sync.dma_start(will_t[:], will)
+        nc.sync.dma_start(peak_t[:], peak)
+
+        w_bf = [keep.tile([P, M, PACK], BF16, name="w_bf%d" % g, align_bytes=64) for g in range(PASSES)]
+        w_codes = [keep.tile([P, M], U32, name="w_codes%d" % g, align_bytes=64) for g in range(PASSES)]
+        w_scales = [keep.tile([P, M], U8, name="w_scales%d" % g, align_bytes=64) for g in range(PASSES)]
+        for g in range(PASSES):
+            nc.scalar.activation(
+                w_bf[g][:].rearrange("p (c i) t -> p c t i", i=4),
+                w_raw[:, g, :, :].rearrange("p t (c i) -> p c t i", i=4),
+                ACT.Copy,
+            )
+
+        got_scales = keep.tile([P, S], U8, name="got_scales", align_bytes=64)
+        got_words0 = keep.tile([P, S], U32, name="got_words0", align_bytes=64)
+        got_words1 = [
+            keep.tile([P, b - a], U32, name="got_words1_%d" % a, align_bytes=64) for a, b in LINK_PIECES
+        ]
+        nc.vector.tensor_copy(got_words0[:], words[0][:].indirect(offs_t[:]))
+        nc.vector.tensor_copy(got_scales[:], scales[:].indirect(offs_t[:]))
+        for g in range(PASSES):
+            nc.vector.quantize_mx(
+                out=w_codes[g][:].bitcast(FP8X4),
+                scales=w_scales[g][:],
+                in_=w_bf[g][:].rearrange("p m t -> p (m t)"),
+            )
+        for piece, got in zip(LINK_PIECES, got_words1):
+            nc.vector.tensor_copy(got[:], words[1][:].indirect(offs_t[:, list_cols(piece)]))
+
+        y = [psum.tile([P, b - a], F32, name="y%d" % a) for a, b in LINK_PIECES]
+        for piece, bank in zip(LINK_PIECES, y):
+            nc.tensor.matmul_mx(
+                out=bank[:],
+                lhsT=w_codes[0][:].bitcast(FP8X4),
+                lhsT_scale=w_scales[0][:],
+                rhs=got_words0[:, cols(piece)].bitcast(FP8X4),
+                rhs_scale=got_scales[:, cols(piece)],
+                start=True,
+                stop=False,
+            )
+        exp_y = keep.tile([P, S], F32, name="exp_y")
+        for piece, bank, got in zip(LINK_PIECES, y, got_words1):
+            nc.tensor.matmul_mx(
+                out=bank[:],
+                lhsT=w_codes[1][:].bitcast(FP8X4),
+                lhsT_scale=w_scales[1][:],
+                rhs=got[:].bitcast(FP8X4),
+                rhs_scale=got_scales[4:P, cols(piece)],
+                start=False,
+                stop=True,
+            )
+            nc.scalar.activation(exp_y[:, cols(piece)], bank[:], ACT.Exp)
+
+        capped = keep.tile([P, S], F32, name="capped", tag="reuse_a")
+        nc.vector.tensor_scalar_min(capped[:], exp_y[:], EXP_CAP)
+        log1p = keep.tile([P, S], F32, name="log1p", tag="reuse_b")
+        softplus = keep.tile([P, S], F32, name="softplus")
+        for piece, bank in zip(LINK_PIECES, y):
+            nc.scalar.activation(log1p[:, cols(piece)], capped[:, cols(piece)], ACT.Ln, bias=1.0)
+            nc.vector.scalar_tensor_tensor(
+                softplus[:, cols(piece)], bank[:], 0.0, log1p[:, cols(piece)], ALU.max, ALU.max
+            )
+
+        ln_will = keep.tile([P, U], F32, name="ln_will", tag="reuse_a")
+        ln_peak = keep.tile([P, U], F32, name="ln_peak", tag="reuse_b")
+        nc.scalar.activation(ln_will[:], will_t[:], ACT.Ln)
+        nc.scalar.activation(ln_peak[:], peak_t[:], ACT.Ln)
+
+        one = keep.tile([P, U], F32, name="one")
+        two = keep.tile([P, U], F32, name="two")
+        three = keep.tile([P, U], F32, name="three")
+        for piece in FLOW_PIECES:
+            nc.vector.tensor_copy(one[:, cols(piece)], softplus[:].indirect(lnk_t[0][:, list_cols(piece)]))
+        for piece in FLOW_PIECES:
+            nc.vector.tensor_tensor(
+                two[:, cols(piece)], softplus[:].indirect(lnk_t[1][:, list_cols(piece)]), one[:, cols(piece)], ALU.add
+            )
+        ln_cost = keep.tile([P, U], F32, name="ln_cost")
+        ln_path = keep.tile([P, U], F32, name="ln_path")
+        for piece in FLOW_PIECES:
+            nc.vector.tensor_tensor(
+                three[:, cols(piece)], softplus[:].indirect(lnk_t[2][:, list_cols(piece)]), two[:, cols(piece)], ALU.add
+            )
+            nc.scalar.activation(ln_cost[:, cols(piece)], three[:, cols(piece)], ACT.Ln, bias=0.1, scale=0.6)
+            nc.scalar.activation(ln_path[:, cols(piece)], three[:, cols(piece)], ACT.Ln, bias=TINY, scale=0.6)
+
+        ln_free = keep.tile([P, U], F32, name="ln_free")
+        ln_rate = keep.tile([P, U], F32, name="ln_rate")
+        ln_paid = keep.tile([P, U], F32, name="ln_paid")
+        gain = keep.tile([P, U], F32, name="gain")
+        paid = keep.tile([P, U], F32, name="paid")
+        result = keep.tile([P, U], F32, name="result")
+        for piece in FLOW_PIECES:
+            c = cols(piece)
+            nc.vector.tensor_tensor(ln_free[:, c], ln_will[:, c], ln_cost[:, c], ALU.subtract)
+        for piece in FLOW_PIECES:
+            c = cols(piece)
+            nc.vector.tensor_tensor(ln_rate[:, c], ln_free[:, c], ln_peak[:, c], ALU.min)
+        for piece in FLOW_PIECES:
+            c = cols(piece)
+            nc.vector.tensor_tensor(ln_paid[:, c], ln_rate[:, c], ln_path[:, c], ALU.add)
+        for piece in FLOW_PIECES:
+            c = cols(piece)
+            nc.vector.tensor_tensor(gain[:, c], ln_rate[:, c], will_t[:, c], ALU.mult)
+        for piece in FLOW_PIECES:
+            c = cols(piece)
+            nc.scalar.activation(paid[:, c], ln_paid[:, c], ACT.Exp)
+            nc.vector.tensor_tensor(result[:, c], gain[:, c], paid[:, c], ALU.subtract)
+            nc.sync.dma_start(out[:, c], result[:, c])

@@ -46,21 +46,25 @@ def tile_picked_ynumdl_util_p_kernel(
 
         offs_t = keep.tile([P, S // PER_COL], U16, name="offs_t")
         lnk_t = [keep.tile([P, U // PER_COL], U16, name="lnk_t%d" % i) for i in range(3)]
-        w_raw = keep.tile([P, PASSES, PACK, M], F32, name="w_raw")
+        w_raw = [keep.tile([P, PACK, M], F32, name="w_raw%d" % g) for g in range(PASSES)]
         words = [keep.tile([P, T], U32, name="words%d" % g, align_bytes=64) for g in range(PASSES)]
         scales = keep.tile([P, T], U8, name="scales", align_bytes=64)
         will_t = keep.tile([P, U], F32, name="will_t")
         peak_t = keep.tile([P, U], F32, name="peak_t")
 
+        def load_w(g):
+            nc.sync.dma_start(w_raw[g][:], w1[g * 512 : (g + 1) * 512, :].rearrange("(p j) m -> p j m", j=PACK))
+
         nc.vector.memset(scales[:].bitcast(I32), 0)
         nc.sync.dma_start(offs_t[:], offs)
-        nc.sync.dma_start(words[0][:].bitcast(I32), x_words[0].rearrange("p n t -> p (n t)").bitcast(I32))
+        load_w(0)
         for q in range(4):
             nc.sync.dma_start(
                 scales[32 * q : 32 * q + 8, :].bitcast(I32), x_scales[:, 4 * q : 4 * q + 4, :].bitcast(I32)
             )
-        nc.sync.dma_start(w_raw[:], w1.rearrange("(g p j) m -> p g j m", g=PASSES, j=PACK))
-        nc.sync.dma_start(words[1][:].bitcast(I32), x_words[1].rearrange("p n t -> p (n t)").bitcast(I32))
+        load_w(1)
+        for g in range(PASSES):
+            nc.sync.dma_start(words[g][:].bitcast(I32), x_words[g].rearrange("p n t -> p (n t)").bitcast(I32))
         for tile, lnk in zip(lnk_t, (lnk1, lnk2, lnk3)):
             nc.sync.dma_start(tile[:], lnk)
         nc.sync.dma_start(will_t[:], will)
@@ -72,7 +76,7 @@ def tile_picked_ynumdl_util_p_kernel(
         for g in range(PASSES):
             nc.scalar.activation(
                 w_bf[g][:].rearrange("p (c i) t -> p c t i", i=4),
-                w_raw[:, g, :, :].rearrange("p t (c i) -> p c t i", i=4),
+                w_raw[g][:].rearrange("p t (c i) -> p c t i", i=4),
                 ACT.Copy,
             )
 
@@ -81,7 +85,6 @@ def tile_picked_ynumdl_util_p_kernel(
         got_words1 = [
             keep.tile([P, b - a], U32, name="got_words1_%d" % a, align_bytes=64) for a, b in LINK_PIECES
         ]
-        nc.vector.tensor_copy(got_words0[:], words[0][:].indirect(offs_t[:]))
         nc.vector.tensor_copy(got_scales[:], scales[:].indirect(offs_t[:]))
         for g in range(PASSES):
             nc.vector.quantize_mx(
@@ -89,6 +92,7 @@ def tile_picked_ynumdl_util_p_kernel(
                 scales=w_scales[g][:],
                 in_=w_bf[g][:].rearrange("p m t -> p (m t)"),
             )
+        nc.vector.tensor_copy(got_words0[:], words[0][:].indirect(offs_t[:]))
         for piece, got in zip(LINK_PIECES, got_words1):
             nc.vector.tensor_copy(got[:], words[1][:].indirect(offs_t[:, list_cols(piece)]))
 

from contextlib import ExitStack

import concourse.mybir as mybir

F32 = mybir.dt.float32
BF16 = mybir.dt.bfloat16
I32 = mybir.dt.int32
U32 = mybir.dt.uint32
U16 = mybir.dt.uint16
U8 = mybir.dt.uint8
FP8X4 = mybir.dt.float8_e4m3fn_x4
ALU = mybir.AluOpType
ACT = mybir.ActivationFunctionType

P = 128
PACK = 4
PASSES = 2
T = 1024
S = 512
U = 512
M = 128
PER_COL = 16
FLOPS = 2 * PASSES * P * PACK * M * S

LINK_PIECES = ((0, 256), (256, 384), (384, 512))
FLOW_PIECES = ((0, 256), (256, 512))
EXP_CAP = 2.0 ** 60
TINY = 1e-18


def cols(piece):
    return slice(piece[0], piece[1])


def list_cols(piece):
    return slice(piece[0] // PER_COL, piece[1] // PER_COL)


def tile_picked_ynumdl_util_p_kernel(
    tc, x_words, x_scales, w1, will, peak, offs, lnk1, lnk2, lnk3, out
):
    nc = tc.nc
    with ExitStack() as ctx:
        keep = ctx.enter_context(tc.tile_pool(name="keep", bufs=1))
        psum = ctx.enter_context(tc.psum_pool(name="psum", bufs=1))

        offs_t = keep.tile([P, S // PER_COL], U16, name="offs_t")
        lnk_t = [keep.tile([P, U // PER_COL], U16, name="lnk_t%d" % i) for i in range(3)]
        w_raw = [keep.tile([P, PACK, M], F32, name="w_raw%d" % g) for g in range(PASSES)]
        words = [keep.tile([P, T], U32, name="words%d" % g, align_bytes=64) for g in range(PASSES)]
        scales = keep.tile([P, T], U8, name="scales", align_bytes=64)
        will_t = keep.tile([P, U], F32, name="will_t")
        peak_t = keep.tile([P, U], F32, name="peak_t")

        def load_w(g):
            nc.sync.dma_start(w_raw[g][:], w1[g * 512 : (g + 1) * 512, :].rearrange("(p j) m -> p j m", j=PACK))

        nc.vector.memset(scales[:].bitcast(I32), 0)
        nc.sync.dma_start(offs_t[:], offs)
        load_w(0)
        for q in range(4):
            nc.sync.dma_start(
                scales[32 * q : 32 * q + 8, :].bitcast(I32), x_scales[:, 4 * q : 4 * q + 4, :].bitcast(I32)
            )
        load_w(1)
        for g in range(PASSES):
            nc.sync.dma_start(words[g][:].bitcast(I32), x_words[g].rearrange("p n t -> p (n t)").bitcast(I32))
        for tile, lnk in zip(lnk_t, (lnk1, lnk2, lnk3)):
            nc.sync.dma_start(tile[:], lnk)
        nc.sync.dma_start(will_t[:], will)
        nc.sync.dma_start(peak_t[:], peak)

        w_bf = [keep.tile([P, M, PACK], BF16, name="w_bf%d" % g, align_bytes=64) for g in range(PASSES)]
        w_codes = [keep.tile([P, M], U32, name="w_codes%d" % g, align_bytes=64) for g in range(PASSES)]
        w_scales = [keep.tile([P, M], U8, name="w_scales%d" % g, align_bytes=64) for g in range(PASSES)]
        for g in range(PASSES):
            nc.scalar.activation(
                w_bf[g][:].rearrange("p (c i) t -> p c t i", i=4),
                w_raw[g][:].rearrange("p t (c i) -> p c t i", i=4),
                ACT.Copy,
            )

        got_scales = keep.tile([P, S], U8, name="got_scales", align_bytes=64)
        got_words0 = keep.tile([P, S], U32, name="got_words0", align_bytes=64)
        got_words1 = [
            keep.tile([P, b - a], U32, name="got_words1_%d" % a, align_bytes=64) for a, b in LINK_PIECES
        ]
        nc.vector.tensor_copy(got_scales[:], scales[:].indirect(offs_t[:]))
        for g in range(PASSES):
            nc.vector.quantize_mx(
                out=w_codes[g][:].bitcast(FP8X4),
                scales=w_scales[g][:],
                in_=w_bf[g][:].rearrange("p m t -> p (m t)"),
            )
        nc.vector.tensor_copy(got_words0[:], words[0][:].indirect(offs_t[:]))
        for piece, got in zip(LINK_PIECES, got_words1):
            nc.vector.tensor_copy(got[:], words[1][:].indirect(offs_t[:, list_cols(piece)]))

        y = [psum.tile([P, b - a], F32, name="y%d" % a) for a, b in LINK_PIECES]
        for piece, bank in zip(LINK_PIECES, y):
            nc.tensor.matmul_mx(
                out=bank[:],
                lhsT=w_codes[0][:].bitcast(FP8X4),
                lhsT_scale=w_scales[0][:],
                rhs=got_words0[:, cols(piece)].bitcast(FP8X4),
                rhs_scale=got_scales[:, cols(piece)],
                start=True,
                stop=False,
            )
        exp_y = keep.tile([P, S], F32, name="exp_y")
        for piece, bank, got in zip(LINK_PIECES, y, got_words1):
            nc.tensor.matmul_mx(
                out=bank[:],
                lhsT=w_codes[1][:].bitcast(FP8X4),
                lhsT_scale=w_scales[1][:],
                rhs=got[:].bitcast(FP8X4),
                rhs_scale=got_scales[4:P, cols(piece)],
                start=False,
                stop=True,
            )
            nc.scalar.activation(exp_y[:, cols(piece)], bank[:], ACT.Exp)

        capped = keep.tile([P, S], F32, name="capped", tag="reuse_a")
        nc.vector.tensor_scalar_min(capped[:], exp_y[:], EXP_CAP)
        log1p = keep.tile([P, S], F32, name="log1p", tag="reuse_b")
        softplus = keep.tile([P, S], F32, name="softplus")
        for piece, bank in zip(LINK_PIECES, y):
            nc.scalar.activation(log1p[:, cols(piece)], capped[:, cols(piece)], ACT.Ln, bias=1.0)
            nc.vector.scalar_tensor_tensor(
                softplus[:, cols(piece)], bank[:], 0.0, log1p[:, cols(piece)], ALU.max, ALU.max
            )

        ln_will = keep.tile([P, U], F32, name="ln_will", tag="reuse_a")
        ln_peak = keep.tile([P, U], F32, name="ln_peak", tag="reuse_b")
        nc.scalar.activation(ln_will[:], will_t[:], ACT.Ln)
        nc.scalar.activation(ln_peak[:], peak_t[:], ACT.Ln)

        one = keep.tile([P, U], F32, name="one")
        two = keep.tile([P, U], F32, name="two")
        three = keep.tile([P, U], F32, name="three")
        for piece in FLOW_PIECES:
            nc.vector.tensor_copy(one[:, cols(piece)], softplus[:].indirect(lnk_t[0][:, list_cols(piece)]))
        for piece in FLOW_PIECES:
            nc.vector.tensor_tensor(
                two[:, cols(piece)], softplus[:].indirect(lnk_t[1][:, list_cols(piece)]), one[:, cols(piece)], ALU.add
            )
        ln_cost = keep.tile([P, U], F32, name="ln_cost")
        ln_path = keep.tile([P, U], F32, name="ln_path")
        for piece in FLOW_PIECES:
            nc.vector.tensor_tensor(
                three[:, cols(piece)], softplus[:].indirect(lnk_t[2][:, list_cols(piece)]), two[:, cols(piece)], ALU.add
            )
            nc.scalar.activation(ln_cost[:, cols(piece)], three[:, cols(piece)], ACT.Ln, bias=0.1, scale=0.6)
            nc.scalar.activation(ln_path[:, cols(piece)], three[:, cols(piece)], ACT.Ln, bias=TINY, scale=0.6)

        ln_free = keep.tile([P, U], F32, name="ln_free")
        ln_rate = keep.tile([P, U], F32, name="ln_rate")
        ln_paid = keep.tile([P, U], F32, name="ln_paid")
        gain = keep.tile([P, U], F32, name="gain")
        paid = keep.tile([P, U], F32, name="paid")
        result = keep.tile([P, U], F32, name="result")
        for piece in FLOW_PIECES:
            c = cols(piece)
            nc.vector.tensor_tensor(ln_free[:, c], ln_will[:, c], ln_cost[:, c], ALU.subtract)
        for piece in FLOW_PIECES:
            c = cols(piece)
            nc.vector.tensor_tensor(ln_rate[:, c], ln_free[:, c], ln_peak[:, c], ALU.min)
        for piece in FLOW_PIECES:
            c = cols(piece)
            nc.vector.tensor_tensor(ln_paid[:, c], ln_rate[:, c], ln_path[:, c], ALU.add)
        for piece in FLOW_PIECES:
            c = cols(piece)
            nc.vector.tensor_tensor(gain[:, c], ln_rate[:, c], will_t[:, c], ALU.mult)
        for piece in FLOW_PIECES:
            c = cols(piece)
            nc.scalar.activation(paid[:, c], ln_paid[:, c], ACT.Exp)
            nc.vector.tensor_tensor(result[:, c], gain[:, c], paid[:, c], ALU.subtract)
            nc.sync.dma_start(out[:, c], result[:, c])
